import numpy as np
import ml_dtypes


def mxq(x, axis, fmt="e4m3"):
    dtype, down = {"e4m3": (ml_dtypes.float8_e4m3fn, 7), "e5m2": (ml_dtypes.float8_e5m2, 14)}[fmt]
    v = np.moveaxis(np.asarray(x, np.float32).astype(ml_dtypes.bfloat16).astype(np.float64), axis, -1)
    blocks = v.reshape(v.shape[:-1] + (-1, 32))
    amax = np.abs(blocks).max(-1, keepdims=True)
    byte = np.maximum(np.where(amax > 0, np.frexp(amax)[1] - 1 + 127, 0) - down, 1)
    scale = np.exp2(byte - 127.0)
    codes = (blocks / scale).astype(np.float32).astype(dtype).astype(np.float64)
    return np.moveaxis((codes * scale).reshape(v.shape), -1, axis)


WIDE = False


def mx_kscale(k):
    if not WIDE:
        return np.ones(k)
    levels = np.array([10, -10, 5, -5, 0])
    if k % 512:
        return np.exp2(np.random.permutation(np.resize(levels, k // 32))).repeat(32)
    a = np.empty((k // 512, 16))
    for p in range(k // 512):
        a[p, :8] = np.random.permutation(np.resize(levels, 8))
        for g in range(8):
            far = levels[np.abs(levels - a[p, g]) >= 10]
            a[p, g + 8] = far[np.random.randint(len(far))]
    return np.exp2(a.ravel()).repeat(32)


def f64(x):
    return np.asarray(x).astype(np.float64)


def striped8(idx):
    return np.asarray(idx).reshape(8, -1, 16).transpose(0, 2, 1).reshape(128, -1).astype(np.uint16)


def unstriped8(offs):
    return offs.reshape(8, 16, -1).transpose(0, 2, 1).reshape(8, -1).astype(np.int64)


def pick8(x, idx, run):
    r = np.arange(len(x))
    return x[r[:, None], idx[r % (8 * run) // run]]


E2M1 = np.array([0.0, 0.5, 1.0, 1.5, 2.0, 3.0, 4.0, 6.0, -0.0, -0.5, -1.0, -1.5, -2.0, -3.0, -4.0, -6.0])


def pack_weight(w, fmt):
    k, n = w.shape
    w = f64(np.asarray(w, np.float32).astype(ml_dtypes.bfloat16)).reshape(k // 32, 32, n)
    amax = np.abs(w).max(1)
    if fmt == "e4m3":
        byte = np.frexp(amax)[1] - 1 + 127 - 7
    else:
        mant, ex = np.frexp(amax / 6.0)
        byte = np.where(mant > 0.5, ex, ex - 1) + 127
    byte = np.clip(np.where(amax > 0, byte, 1), 1, 254)
    scaled = (w * np.exp2(127.0 - byte)[:, None, :]).reshape(k, n).astype(np.float32)
    by_word = np.ascontiguousarray(scaled.reshape(k // 512, 128, 4, n).transpose(0, 1, 3, 2))
    if fmt == "e4m3":
        words = by_word.astype(ml_dtypes.float8_e4m3fn).view(np.uint8)
    else:
        c = by_word.astype(ml_dtypes.float4_e2m1fn).view(np.uint8) & 0xF
        words = (c[..., 0::2] | (c[..., 1::2] << 4)).reshape(k // 512, 128, 2 * n)
    return np.ascontiguousarray(words), np.ascontiguousarray(byte.astype(np.uint8).reshape(k // 512, 16, n))


def unpack_weight(words, scales, fmt):
    g, _, n = scales.shape
    words = np.ascontiguousarray(words).reshape(g, 128, n, -1)
    if fmt == "e4m3":
        vals = words.view(ml_dtypes.float8_e4m3fn).astype(np.float64)
    else:
        nib = np.empty((g, 128, n, 4), np.uint8)
        nib[..., 0::2] = words & 0xF
        nib[..., 1::2] = words >> 4
        vals = E2M1[nib]
    vals = vals * np.repeat(np.exp2(scales.astype(np.float64) - 127.0), 8, axis=1)[..., None]
    return vals.transpose(0, 1, 3, 2).reshape(g * 512, n)


D, V, Q, I = 512, 2048, 128, 512


def setup_inputs():
    n = np.random.standard_normal
    idx = np.stack([np.random.permutation(V)[:I] for _ in range(8)])
    idx2 = np.stack([np.random.permutation(V)[:I] for _ in range(8)])
    fd = mx_kscale(D)
    vocp = pack_weight(n((D, V)) / fd[:, None], "e2m1")
    return {
        "hid": (n((D, Q)) * 0.8 / np.sqrt(D) * fd[:, None]).astype(np.float32),
        "voc_words": vocp[0],
        "voc_scales": vocp[1],
        "target": (np.random.uniform(0.0, 2.0, (Q, I))).astype(np.float32),
        "base": (0.3 * n((Q, V))).astype(np.float32),
        "offs": striped8(idx),
        "offs2": striped8(idx2),
    }


def reference(hid, voc_words, voc_scales, target, base, offs, offs2):
    idx = unstriped8(offs)
    idx2 = unstriped8(offs2)
    vocu = unpack_weight(voc_words, voc_scales, "e2m1")
    hidq = mxq(f64(hid), 0, "e4m3")
    a = hidq.T @ vocu
    p = np.exp(pick8(a, idx, 16))
    z = np.sum(p, axis=1, keepdims=True)
    b = np.exp(pick8(a, idx2, 16)) / z * 512.0
    db = f64(target) / (b + 1.0)
    dz = np.sum(db * 512.0 * np.exp(pick8(a, idx2, 16)) / np.square(z) * (-1.0), axis=1, keepdims=True)
    e1 = db * 512.0 / z * np.exp(pick8(a, idx2, 16))
    s1 = np.zeros((Q, V))
    s1[np.arange(Q)[:, None], idx2[np.arange(Q) % 128 // 16]] = e1
    e2 = dz * p
    s2 = np.zeros((Q, V))
    s2[np.arange(Q)[:, None], idx[np.arange(Q) % 128 // 16]] = e2
    da = s1 + s2
    hda = da * 2.0
    he2 = pick8(hda, idx, 16)
    he1 = pick8(hda, idx2, 16)
    hdz = np.sum(he2 * p, axis=1, keepdims=True)
    hdb = he1 * np.exp(pick8(a, idx2, 16)) / z * 512.0 + hdz * (-1.0) / np.square(z) * np.exp(pick8(a, idx2, 16)) * 512.0
    hb = hdb * f64(target) / np.square(b + 1.0) * (-1.0)
    hz = np.sum(he1 * np.exp(pick8(a, idx2, 16)) * db * 512.0 / np.square(z) * (-1.0), axis=1, keepdims=True) + np.sum(hdz * (-1.0) * db * 512.0 * np.exp(pick8(a, idx2, 16)) / np.square(np.square(z)) * (-1.0), axis=1, keepdims=True) * z * 2.0 + np.sum(hb * 512.0 * np.exp(pick8(a, idx2, 16)) / np.square(z) * (-1.0), axis=1, keepdims=True)
    hp = he2 * dz + hz
    e51 = he1 * db * 512.0 / z * np.exp(pick8(a, idx2, 16))
    s51 = np.zeros((Q, V))
    s51[np.arange(Q)[:, None], idx2[np.arange(Q) % 128 // 16]] = e51
    e52 = hdz * (-1.0) / np.square(z) * db * 512.0 * np.exp(pick8(a, idx2, 16))
    s52 = np.zeros((Q, V))
    s52[np.arange(Q)[:, None], idx2[np.arange(Q) % 128 // 16]] = e52
    e53 = hb * 512.0 / z * np.exp(pick8(a, idx2, 16))
    s53 = np.zeros((Q, V))
    s53[np.arange(Q)[:, None], idx2[np.arange(Q) % 128 // 16]] = e53
    e54 = hp * p
    s54 = np.zeros((Q, V))
    s54[np.arange(Q)[:, None], idx[np.arange(Q) % 128 // 16]] = e54
    ha = s51 + s52 + s53 + s54
    y = ha + f64(base)
    return y

@@ -1,0 +1,227 @@
+import math
+from contextlib import ExitStack
+
+import concourse.mybir as mybir
+from concourse.masks import make_identity
+
+D, V, Q, I = 512, 2048, 128, 512
+FLOPS = 2 * D * Q * V
+
+F32 = mybir.dt.float32
+BF16 = mybir.dt.bfloat16
+I32 = mybir.dt.int32
+U32 = mybir.dt.uint32
+U16 = mybir.dt.uint16
+U8 = mybir.dt.uint8
+FP8X4 = mybir.dt.float8_e4m3fn_x4
+FP4X4 = mybir.dt.float4_e2m1fn_x4
+ALU = mybir.AluOpType
+ACT = mybir.ActivationFunctionType
+
+P = 128
+PACK = 4
+BANK = 512
+BANKS = V // BANK
+BLOCKS = BANK // P
+LN2 = math.log(2.0)
+BITS_SLOPE = LN2 / 2.0**23
+BITS_OFFSET = LN2 * (127.0 + 9.0 - 0.043)
+
+
+def tile_attend_gpallowed_heads_kernel(tc, hid, voc_words, voc_scales, target, base, offs, offs2, out):
+    nc = tc.nc
+    with ExitStack() as ctx:
+        held = ctx.enter_context(tc.tile_pool(name="held", bufs=1))
+        psum = ctx.enter_context(tc.psum_pool(name="psum", bufs=1))
+
+        def wide(name):
+            return held.tile([P, V], F32, name=name)
+
+        def listed(name):
+            return held.tile([P, I], F32, name=name)
+
+        def column(name):
+            return held.tile([P, 1], F32, name=name)
+
+        list1 = held.tile([P, I // 16], U16, name="list1")
+        list2 = held.tile([P, I // 16], U16, name="list2")
+        hid_raw = held.tile([P, PACK, Q], F32, name="hid_raw")
+        word_cuts = [(0, 1024), (1024, 2048)]
+        words = [held.tile([P, 2 * (c1 - c0)], U8, name="words%d" % c0, tag="words%d" % c0, align_bytes=64) for c0, c1 in word_cuts]
+        voc_plane = held.tile([P, V], U8, name="voc_plane", align_bytes=64)
+
+        nc.sync.dma_start(out=hid_raw[:], in_=hid.rearrange("(p t) q -> p t q", t=PACK))
+        for quad in range(4):
+            nc.scalar.dma_start(
+                out=voc_plane[32 * quad : 32 * quad + 4, :].bitcast(I32),
+                in_=voc_scales[0, 4 * quad : 4 * quad + 4, :].bitcast(I32),
+            )
+        for tile, (c0, c1) in zip(words, word_cuts):
+            nc.sync.dma_start(out=tile[:].bitcast(I32), in_=voc_words[0, :, 2 * c0 : 2 * c1].bitcast(I32))
+        nc.sync.dma_start(list1[:], offs)
+        nc.sync.dma_start(list2[:], offs2)
+
+        warm = column("warm")
+        nc.vector.memset(warm[:], 0.0)
+        warm_out = column("warm_out")
+        nc.scalar.activation(warm_out[:], warm[:], ACT.Exp)
+
+        window1 = wide("window1")
+        nc.vector.memset(window1[:].bitcast(U32), 0)
+        identity = held.tile([P, P], F32, name="identity")
+        make_identity(nc, identity[:])
+
+        grouped = held.tile([P, Q, PACK], BF16, name="grouped", tag="grouped_then_window", align_bytes=64)
+        nc.vector.tensor_copy(out=grouped[:], in_=hid_raw[:].rearrange("p t q -> p q t"))
+        hid_codes = held.tile([P, Q], U32, name="hid_codes", tag="codes_then_target", align_bytes=64)
+        hid_plane = held.tile([P, Q], U8, name="hid_plane", align_bytes=64)
+        nc.vector.quantize_mx(
+            out=hid_codes[:].bitcast(FP8X4), scales=hid_plane[:], in_=grouped[:].rearrange("p q t -> p (q t)")
+        )
+
+        window2 = held.tile([P, V], F32, name="window2", tag="grouped_then_window", align_bytes=64)
+        nc.vector.memset(window2[:].bitcast(U32), 0)
+
+        upright = [psum.tile([P, BANK], F32, name="upright%d" % j) for j in range(BANKS)]
+        turned = [psum.tile([P, BANK], F32, name="turned%d" % j) for j in range(BANKS)]
+        a = wide("a")
+        passes = [
+            (0, 512, 0, upright[0], "scalar"),
+            (512, 512, 0, upright[1], "scalar"),
+            (1024, 512, 1, upright[2], "vector"),
+            (1536, 256, 1, upright[3], "scalar"),
+            (1792, 256, 1, turned[3], "vector"),
+        ]
+        for c0, width, piece, bank, engine in passes:
+            w0 = 2 * (c0 - word_cuts[piece][0])
+            nc.tensor.matmul_mx(
+                out=bank[:, :width],
+                lhsT=hid_codes[:].bitcast(FP8X4),
+                lhsT_scale=hid_plane[:],
+                rhs=words[piece][:, w0 : w0 + 2 * width].bitcast(FP4X4),
+                rhs_scale=voc_plane[:, c0 : c0 + width],
+                start=True,
+                stop=True,
+            )
+            if engine == "scalar":
+                nc.scalar.copy(a[:, c0 : c0 + width], bank[:, :width])
+            else:
+                nc.vector.tensor_copy(a[:, c0 : c0 + width], bank[:, :width])
+
+        tgt = held.tile([P, I], F32, name="tgt", tag="codes_then_target", align_bytes=64)
+        nc.sync.dma_start(out=tgt[:], in_=target)
+        base_sb = held.tile([P, V], F32, name="base_sb", tag="words1024", align_bytes=64)
+        nc.sync.dma_start(out=base_sb[:], in_=base)
+
+        for j in range(BANKS):
+            for b in range(BLOCKS):
+                c0 = j * BANK + b * P
+                nc.tensor.matmul(
+                    turned[j][:, b * P : (b + 1) * P], base_sb[:, c0 : c0 + P], identity[:],
+                    start=(b == 0), stop=False, is_transpose=True,
+                )
+
+        a1 = listed("a1")
+        a2 = listed("a2")
+        neg_max = column("neg_max")
+        nc.vector.tensor_copy(a1[:], a[:].indirect(list1[:]))
+        nc.vector.tensor_reduce(neg_max[:], a1[:], mybir.AxisListType.X, ALU.max, negate=True)
+        nc.vector.tensor_copy(a2[:], a[:].indirect(list2[:]))
+
+        p = listed("p")
+        z = column("z")
+        nc.scalar.activation(p[:], a1[:], ACT.Exp, bias=neg_max[:], accum_out=z[:])
+        nc.vector.tensor_copy(window1[:].indirect(list1[:]), p[:])
+
+        k1 = column("k1")
+        nc.scalar.activation(k1[:], neg_max[:], ACT.Copy, scale=0.5, bias=-0.25)
+        z_bits = z[:].bitcast(U32)
+        exp0 = column("exp0")
+        nc.scalar.activation(exp0[:], z_bits, ACT.Exp, scale=-BITS_SLOPE, bias=BITS_OFFSET)
+        zq = column("zq")
+        nc.scalar.activation(zq[:], z[:], ACT.Copy, scale=0.5 / 512.0)
+        n0 = column("n0")
+        nc.scalar.activation(n0[:], z_bits, ACT.Copy, scale=-BITS_SLOPE, bias=BITS_OFFSET - 0.5)
+        h0 = column("h0")
+        nc.scalar.activation(h0[:], exp0[:], ACT.Square, scale=zq[:], bias=-1.0)
+        k2 = column("k2")
+        nc.scalar.activation(k2[:], n0[:], ACT.Identity, scale=0.5, bias=k1[:])
+        exp1 = column("exp1")
+        nc.scalar.activation(exp1[:], h0[:], ACT.Exp, scale=2.0, bias=n0[:])
+        k3 = column("k3")
+        nc.scalar.activation(k3[:], h0[:], ACT.Identity, bias=k2[:])
+        h1 = column("h1")
+        nc.scalar.activation(h1[:], exp1[:], ACT.Square, scale=zq[:], bias=-1.0)
+        shift = column("shift")
+        nc.scalar.activation(shift[:], h1[:], ACT.Identity, bias=k3[:])
+        th = listed("th")
+        nc.scalar.activation(th[:], a2[:], ACT.Tanh, scale=0.5, bias=shift[:])
+        neg_z = column("neg_z")
+        nc.scalar.activation(neg_z[:], z[:], ACT.Copy, scale=-1.0)
+        half_r = listed("half_r")
+        nc.scalar.activation(half_r[:], th[:], ACT.Identity, scale=-0.25, bias=0.25)
+
+        e1x2 = listed("e1x2")
+        sum_e1x2 = column("sum_e1x2")
+        nc.vector.scalar_tensor_tensor(e1x2[:], th[:], 1.0, tgt[:], ALU.add, ALU.mult, accum_out=sum_e1x2[:])
+        neg_rz = column("neg_rz")
+        nc.vector.reciprocal(neg_rz[:], neg_z[:])
+        nc.vector.tensor_copy(window2[:].indirect(list2[:]), e1x2[:])
+        w = listed("w")
+        sum_w = column("sum_w")
+        nc.vector.scalar_tensor_tensor(w[:], e1x2[:], 1.0, half_r[:], ALU.mult, ALU.mult, accum_out=sum_w[:])
+
+        dz_x2 = column("dz_x2")
+        nc.scalar.activation(dz_x2[:], sum_e1x2[:], ACT.Copy, scale=neg_rz[:])
+        sum_e1 = column("sum_e1")
+        nc.scalar.activation(sum_e1[:], sum_e1x2[:], ACT.Copy, scale=0.5)
+        both = column("both")
+        nc.scalar.activation(both[:], sum_w[:], ACT.Identity, bias=sum_e1[:])
+        both_rz = column("both_rz")
+        nc.scalar.activation(both_rz[:], both[:], ACT.Copy, scale=neg_rz[:])
+
+        hda = wide("hda")
+        nc.vector.scalar_tensor_tensor(hda[:], window1[:], dz_x2[:], window2[:], ALU.mult, ALU.add)
+
+        he2_p = listed("he2_p")
+        nc.vector.tensor_tensor(he2_p[:], hda[:].indirect(list1[:]), p[:], ALU.mult)
+        he1_w = listed("he1_w")
+        nc.vector.tensor_tensor(he1_w[:], hda[:].indirect(list2[:]), w[:], ALU.mult)
+
+        neg_he2_pn = listed("neg_he2_pn")
+        neg_h = column("neg_h")
+        nc.scalar.activation(neg_he2_pn[:], he2_p[:], ACT.Copy, scale=neg_rz[:], accum_out=neg_h[:])
+        neg_h_w = listed("neg_h_w")
+        nc.scalar.activation(neg_h_w[:], w[:], ACT.Copy, scale=neg_h[:])
+        nc.vector.tensor_tensor(window2[:].indirect(list2[:]), he1_w[:], neg_h_w[:], ALU.add)
+
+        scaled = listed("scaled")
+        u = column("u")
+        nc.scalar.activation(scaled[:], he1_w[:], ACT.Copy, scale=neg_rz[:], accum_out=u[:])
+        hz = column("hz")
+        nc.scalar.activation(hz[:], neg_h[:], ACT.Identity, scale=both_rz[:], bias=u[:])
+        hz_p = listed("hz_p")
+        nc.scalar.activation(hz_p[:], p[:], ACT.Copy, scale=hz[:])
+        he2_dz_p = listed("he2_dz_p")
+        nc.scalar.activation(he2_dz_p[:], neg_he2_pn[:], ACT.Copy, scale=sum_e1[:])
+        nc.vector.tensor_tensor(window1[:].indirect(list1[:]), he2_dz_p[:], hz_p[:], ALU.add)
+
+        for j in range(BANKS):
+            for b in range(BLOCKS):
+                c0 = j * BANK + b * P
+                nc.tensor.matmul(
+                    turned[j][:, b * P : (b + 1) * P], window2[:, c0 : c0 + P], identity[:],
+                    start=False, stop=(b == BLOCKS - 1), is_transpose=True,
+                )
+        for j in range(BANKS):
+            staged = held.tile([P, BANK], F32, name="staged%d" % j)
+            nc.scalar.copy(staged[:], turned[j][:])
+            for b in range(BLOCKS):
+                nc.tensor.transpose(upright[j][:, b * P : (b + 1) * P], staged[:, b * P : (b + 1) * P], identity[:])
+        pieces = [(0, 512), (512, 512), (1024, 512), (1536, 256), (1792, 256)]
+        for n, (c0, width) in enumerate(pieces):
+            result = held.tile([P, width], F32, name="result%d" % n)
+            cols = slice(c0, c0 + width)
+            nc.vector.tensor_tensor(result[:], upright[c0 // BANK][:, c0 % BANK : c0 % BANK + width], window1[:, cols], ALU.add)
+            queue = nc.sync if n % 2 == 0 else nc.scalar
+            queue.dma_start(out=out[:, cols], in_=result[:])

@@ -113,25 +113,31 @@ def tile_attend_gpallowed_heads_kernel(tc, hid, voc_words, voc_scales, target, b
         base_sb = held.tile([P, V], F32, name="base_sb", tag="words1024", align_bytes=64)
         nc.sync.dma_start(out=base_sb[:], in_=base)
 
-        for j in range(BANKS):
-            for b in range(BLOCKS):
-                c0 = j * BANK + b * P
-                nc.tensor.matmul(
-                    turned[j][:, b * P : (b + 1) * P], base_sb[:, c0 : c0 + P], identity[:],
-                    start=(b == 0), stop=False, is_transpose=True,
-                )
-
         a1 = listed("a1")
-        a2 = listed("a2")
+        a2 = held.tile([P, I], F32, name="a2", tag="a2_then_staged")
         neg_max = column("neg_max")
         nc.vector.tensor_copy(a1[:], a[:].indirect(list1[:]))
         nc.vector.tensor_reduce(neg_max[:], a1[:], mybir.AxisListType.X, ALU.max, negate=True)
         nc.vector.tensor_copy(a2[:], a[:].indirect(list2[:]))
 
-        p = listed("p")
+        p = held.tile([P, I], F32, name="p", tag="p_then_staged")
         z = column("z")
         nc.scalar.activation(p[:], a1[:], ACT.Exp, bias=neg_max[:], accum_out=z[:])
         nc.vector.tensor_copy(window1[:].indirect(list1[:]), p[:])
+
+        def turn_in(source, j, opens, closes, blocks=BLOCKS):
+            for b in range(blocks):
+                c0 = j * BANK + b * P
+                nc.tensor.matmul(
+                    turned[j][:, b * P : (b + 1) * P], source[:, c0 : c0 + P], identity[:],
+                    start=(opens and b == 0), stop=(closes and b == blocks - 1), is_transpose=True,
+                )
+
+        def turn_back(j, staged, blocks=BLOCKS):
+            nc.scalar.copy(staged[:, j * BANK : j * BANK + blocks * P], turned[j][:, : blocks * P])
+            for b in range(blocks):
+                c0 = j * BANK + b * P
+                nc.tensor.transpose(upright[j][:, b * P : (b + 1) * P], staged[:, c0 : c0 + P], identity[:])
 
         k1 = column("k1")
         nc.scalar.activation(k1[:], neg_max[:], ACT.Copy, scale=0.5, bias=-0.25)
@@ -152,12 +158,12 @@ def tile_attend_gpallowed_heads_kernel(tc, hid, voc_words, voc_scales, target, b
         nc.scalar.activation(k3[:], h0[:], ACT.Identity, bias=k2[:])
         h1 = column("h1")
         nc.scalar.activation(h1[:], exp1[:], ACT.Square, scale=zq[:], bias=-1.0)
+        neg_z = column("neg_z")
+        nc.scalar.activation(neg_z[:], z[:], ACT.Copy, scale=-1.0)
         shift = column("shift")
         nc.scalar.activation(shift[:], h1[:], ACT.Identity, bias=k3[:])
         th = listed("th")
         nc.scalar.activation(th[:], a2[:], ACT.Tanh, scale=0.5, bias=shift[:])
-        neg_z = column("neg_z")
-        nc.scalar.activation(neg_z[:], z[:], ACT.Copy, scale=-1.0)
         half_r = listed("half_r")
         nc.scalar.activation(half_r[:], th[:], ACT.Identity, scale=-0.25, bias=0.25)
 
@@ -167,21 +173,33 @@ def tile_attend_gpallowed_heads_kernel(tc, hid, voc_words, voc_scales, target, b
         neg_rz = column("neg_rz")
         nc.vector.reciprocal(neg_rz[:], neg_z[:])
         nc.vector.tensor_copy(window2[:].indirect(list2[:]), e1x2[:])
-        w = listed("w")
-        sum_w = column("sum_w")
-        nc.vector.scalar_tensor_tensor(w[:], e1x2[:], 1.0, half_r[:], ALU.mult, ALU.mult, accum_out=sum_w[:])
 
         dz_x2 = column("dz_x2")
         nc.scalar.activation(dz_x2[:], sum_e1x2[:], ACT.Copy, scale=neg_rz[:])
         sum_e1 = column("sum_e1")
         nc.scalar.activation(sum_e1[:], sum_e1x2[:], ACT.Copy, scale=0.5)
-        both = column("both")
-        nc.scalar.activation(both[:], sum_w[:], ACT.Identity, bias=sum_e1[:])
-        both_rz = column("both_rz")
-        nc.scalar.activation(both_rz[:], both[:], ACT.Copy, scale=neg_rz[:])
+
+        staged_p = held.tile([P, V - BANK], F32, name="staged_p", tag="a2_then_staged")
+        for j in range(BANKS - 1):
+            turn_in(window1, j, True, True)
+        for j in range(BANKS - 1):
+            turn_back(j, staged_p)
 
         hda = wide("hda")
-        nc.vector.scalar_tensor_tensor(hda[:], window1[:], dz_x2[:], window2[:], ALU.mult, ALU.add)
+        last = slice(V - BANK, V)
+        s2_last = held.tile([P, BANK], F32, name="s2_last")
+        nc.scalar.activation(s2_last[:], window1[:, last], ACT.Copy, scale=dz_x2[:])
+        nc.gpsimd.tensor_tensor(hda[:, last], s2_last[:], window2[:, last], ALU.add)
+        for j in range(BANKS - 1):
+            cols = slice(j * BANK, (j + 1) * BANK)
+            nc.vector.scalar_tensor_tensor(hda[:, cols], upright[j][:], dz_x2[:], window2[:, cols], ALU.mult, ALU.add)
+        w = listed("w")
+        nc.vector.tensor_tensor(w[:], e1x2[:], half_r[:], ALU.mult)
+        dz = column("dz")
+        nc.scalar.activation(dz[:], dz_x2[:], ACT.Copy, scale=0.5)
+        blocks = [4, 4, 4, 4]
+        for j in range(BANKS):
+            turn_in(base_sb, j, True, False, blocks[j])
 
         he2_p = listed("he2_p")
         nc.vector.tensor_tensor(he2_p[:], hda[:].indirect(list1[:]), p[:], ALU.mult)
@@ -191,34 +209,26 @@ def tile_attend_gpallowed_heads_kernel(tc, hid, voc_words, voc_scales, target, b
         neg_he2_pn = listed("neg_he2_pn")
         neg_h = column("neg_h")
         nc.scalar.activation(neg_he2_pn[:], he2_p[:], ACT.Copy, scale=neg_rz[:], accum_out=neg_h[:])
-        neg_h_w = listed("neg_h_w")
-        nc.scalar.activation(neg_h_w[:], w[:], ACT.Copy, scale=neg_h[:])
-        nc.vector.tensor_tensor(window2[:].indirect(list2[:]), he1_w[:], neg_h_w[:], ALU.add)
-
-        scaled = listed("scaled")
-        u = column("u")
-        nc.scalar.activation(scaled[:], he1_w[:], ACT.Copy, scale=neg_rz[:], accum_out=u[:])
-        hz = column("hz")
-        nc.scalar.activation(hz[:], neg_h[:], ACT.Identity, scale=both_rz[:], bias=u[:])
-        hz_p = listed("hz_p")
-        nc.scalar.activation(hz_p[:], p[:], ACT.Copy, scale=hz[:])
         he2_dz_p = listed("he2_dz_p")
         nc.scalar.activation(he2_dz_p[:], neg_he2_pn[:], ACT.Copy, scale=sum_e1[:])
+        hz_part = column("hz_part")
+        nc.scalar.activation(hz_part[:], neg_h[:], ACT.Copy, scale=dz[:])
+        e5 = listed("e5")
+        sum_e5 = column("sum_e5")
+        nc.vector.scalar_tensor_tensor(e5[:], w[:], neg_h[:], he1_w[:], ALU.mult, ALU.add, accum_out=sum_e5[:])
+        nc.vector.tensor_copy(window2[:].indirect(list2[:]), e5[:])
+        hz = column("hz")
+        nc.scalar.activation(hz[:], sum_e5[:], ACT.Identity, scale=neg_rz[:], bias=hz_part[:])
+        hz_p = listed("hz_p")
+        nc.scalar.activation(hz_p[:], p[:], ACT.Copy, scale=hz[:])
         nc.vector.tensor_tensor(window1[:].indirect(list1[:]), he2_dz_p[:], hz_p[:], ALU.add)
 
+        staged_sum = held.tile([P, V], F32, name="staged_sum", tag="p_then_staged")
         for j in range(BANKS):
-            for b in range(BLOCKS):
-                c0 = j * BANK + b * P
-                nc.tensor.matmul(
-                    turned[j][:, b * P : (b + 1) * P], window2[:, c0 : c0 + P], identity[:],
-                    start=False, stop=(b == BLOCKS - 1), is_transpose=True,
-                )
+            turn_in(window2, j, False, True)
         for j in range(BANKS):
-            staged = held.tile([P, BANK], F32, name="staged%d" % j)
-            nc.scalar.copy(staged[:], turned[j][:])
-            for b in range(BLOCKS):
-                nc.tensor.transpose(upright[j][:, b * P : (b + 1) * P], staged[:, b * P : (b + 1) * P], identity[:])
-        pieces = [(0, 512), (512, 512), (1024, 512), (1536, 256), (1792, 256)]
+            turn_back(j, staged_sum)
+        pieces = [(0, 256), (256, 256), (512, 512), (1024, 512), (1536, 256), (1792, 256)]
         for n, (c0, width) in enumerate(pieces):
             result = held.tile([P, width], F32, name="result%d" % n)
             cols = slice(c0, c0 + width)

@@ -158,14 +158,12 @@ def tile_attend_gpallowed_heads_kernel(tc, hid, voc_words, voc_scales, target, b
         nc.scalar.activation(k3[:], h0[:], ACT.Identity, bias=k2[:])
         h1 = column("h1")
         nc.scalar.activation(h1[:], exp1[:], ACT.Square, scale=zq[:], bias=-1.0)
-        neg_z = column("neg_z")
+        neg_z = held.tile([P, 1], F32, name="neg_z", tag="neg_z_then_half_r")
         nc.scalar.activation(neg_z[:], z[:], ACT.Copy, scale=-1.0)
         shift = column("shift")
         nc.scalar.activation(shift[:], h1[:], ACT.Identity, bias=k3[:])
         th = listed("th")
         nc.scalar.activation(th[:], a2[:], ACT.Tanh, scale=0.5, bias=shift[:])
-        half_r = listed("half_r")
-        nc.scalar.activation(half_r[:], th[:], ACT.Identity, scale=-0.25, bias=0.25)
 
         e1x2 = listed("e1x2")
         sum_e1x2 = column("sum_e1x2")
@@ -174,6 +172,10 @@ def tile_attend_gpallowed_heads_kernel(tc, hid, voc_words, voc_scales, target, b
         nc.vector.reciprocal(neg_rz[:], neg_z[:])
         nc.vector.tensor_copy(window2[:].indirect(list2[:]), e1x2[:])
 
+        half_r = held.tile([P, I], F32, name="half_r", tag="neg_z_then_half_r")
+        nc.scalar.activation(half_r[:], th[:], ACT.Identity, scale=-0.25, bias=0.25)
+        w = listed("w")
+        nc.gpsimd.tensor_tensor(w[:], e1x2[:], half_r[:], ALU.mult)
         dz_x2 = column("dz_x2")
         nc.scalar.activation(dz_x2[:], sum_e1x2[:], ACT.Copy, scale=neg_rz[:])
         sum_e1 = column("sum_e1")
@@ -193,8 +195,6 @@ def tile_attend_gpallowed_heads_kernel(tc, hid, voc_words, voc_scales, target, b
         for j in range(BANKS - 1):
             cols = slice(j * BANK, (j + 1) * BANK)
             nc.vector.scalar_tensor_tensor(hda[:, cols], upright[j][:], dz_x2[:], window2[:, cols], ALU.mult, ALU.add)
-        w = listed("w")
-        nc.vector.tensor_tensor(w[:], e1x2[:], half_r[:], ALU.mult)
         dz = column("dz")
         nc.scalar.activation(dz[:], dz_x2[:], ACT.Copy, scale=0.5)
         blocks = [4, 4, 4, 4]

@@ -52,7 +52,7 @@ def tile_attend_gpallowed_heads_kernel(tc, hid, voc_words, voc_scales, target, b
 
         nc.sync.dma_start(out=hid_raw[:], in_=hid.rearrange("(p t) q -> p t q", t=PACK))
         for quad in range(4):
-            nc.scalar.dma_start(
+            nc.sync.dma_start(
                 out=voc_plane[32 * quad : 32 * quad + 4, :].bitcast(I32),
                 in_=voc_scales[0, 4 * quad : 4 * quad + 4, :].bitcast(I32),
             )
@@ -181,23 +181,24 @@ def tile_attend_gpallowed_heads_kernel(tc, hid, voc_words, voc_scales, target, b
         sum_e1 = column("sum_e1")
         nc.scalar.activation(sum_e1[:], sum_e1x2[:], ACT.Copy, scale=0.5)
 
-        staged_p = held.tile([P, V - BANK], F32, name="staged_p", tag="a2_then_staged")
-        for j in range(BANKS - 1):
-            turn_in(window1, j, True, True)
-        for j in range(BANKS - 1):
-            turn_back(j, staged_p)
+        hda_blocks = [4, 4, 3]
+        staged_p = held.tile([P, sum(hda_blocks) * P], F32, name="staged_p", tag="a2_then_staged")
+        for j, n in enumerate(hda_blocks):
+            turn_in(window1, j, True, True, n)
+        for j, n in enumerate(hda_blocks):
+            turn_back(j, staged_p, n)
 
         hda = wide("hda")
-        last = slice(V - BANK, V)
-        s2_last = held.tile([P, BANK], F32, name="s2_last")
+        last = slice(sum(hda_blocks) * P, V)
+        s2_last = held.tile([P, V - sum(hda_blocks) * P], F32, name="s2_last")
         nc.scalar.activation(s2_last[:], window1[:, last], ACT.Copy, scale=dz_x2[:])
         nc.gpsimd.tensor_tensor(hda[:, last], s2_last[:], window2[:, last], ALU.add)
-        for j in range(BANKS - 1):
-            cols = slice(j * BANK, (j + 1) * BANK)
-            nc.vector.scalar_tensor_tensor(hda[:, cols], upright[j][:], dz_x2[:], window2[:, cols], ALU.mult, ALU.add)
+        for j, n in enumerate(hda_blocks):
+            cols = slice(j * BANK, j * BANK + n * P)
+            nc.vector.scalar_tensor_tensor(hda[:, cols], upright[j][:, : n * P], dz_x2[:], window2[:, cols], ALU.mult, ALU.add)
         dz = column("dz")
         nc.scalar.activation(dz[:], dz_x2[:], ACT.Copy, scale=0.5)
-        blocks = [4, 4, 4, 4]
+        blocks = [4, 4, 4, 1]
         for j in range(BANKS):
             turn_in(base_sb, j, True, False, blocks[j])
 
@@ -225,13 +226,20 @@ def tile_attend_gpallowed_heads_kernel(tc, hid, voc_words, voc_scales, target, b
 
         staged_sum = held.tile([P, V], F32, name="staged_sum", tag="p_then_staged")
         for j in range(BANKS):
-            turn_in(window2, j, False, True)
+            turn_in(window2, j, False, True, blocks[j])
         for j in range(BANKS):
-            turn_back(j, staged_sum)
-        pieces = [(0, 256), (256, 256), (512, 512), (1024, 512), (1536, 256), (1792, 256)]
+            turn_back(j, staged_sum, blocks[j])
+        tail = slice(sum(blocks) * P, V)
+        tail_width = V - sum(blocks) * P
+        tail_sum = held.tile([P, tail_width], F32, name="tail_sum")
+        nc.gpsimd.tensor_tensor(tail_sum[:], window2[:, tail], base_sb[:, tail], ALU.add)
+        tail_out = held.tile([P, tail_width], F32, name="tail_out")
+        nc.gpsimd.tensor_tensor(tail_out[:], tail_sum[:], window1[:, tail], ALU.add)
+        pieces = [(0, 256), (256, 256), (512, 512), (1024, 512), (1536, 128)]
         for n, (c0, width) in enumerate(pieces):
             result = held.tile([P, width], F32, name="result%d" % n)
             cols = slice(c0, c0 + width)
             nc.vector.tensor_tensor(result[:], upright[c0 // BANK][:, c0 % BANK : c0 % BANK + width], window1[:, cols], ALU.add)
             queue = nc.sync if n % 2 == 0 else nc.scalar
             queue.dma_start(out=out[:, cols], in_=result[:])
+        nc.scalar.dma_start(out=out[:, tail], in_=tail_out[:])

@@ -21,11 +21,15 @@ ACT = mybir.ActivationFunctionType
 P = 128
 PACK = 4
 BANK = 512
-BANKS = V // BANK
-BLOCKS = BANK // P
-LN2 = math.log(2.0)
-BITS_SLOPE = LN2 / 2.0**23
-BITS_OFFSET = LN2 * (127.0 + 9.0 - 0.043)
+B_FACTOR = 512.0
+
+BITS_SLOPE = math.log(2.0) / 2.0**23
+BITS_OFFSET = math.log(2.0) * (127.0 - 0.043) + math.log(B_FACTOR)
+
+WORD_LOADS = [(0, 512), (512, 1024), (1024, 2048)]
+HDA_BLOCKS = [4, 4, 3]
+OUT_BLOCKS = [4, 4, 4, 1]
+OUT_PIECES = [(0, 256), (256, 256), (512, 512), (1024, 512), (1536, 128)]
 
 
 def tile_attend_gpallowed_heads_kernel(tc, hid, voc_words, voc_scales, target, base, offs, offs2, out):
@@ -34,212 +38,198 @@ def tile_attend_gpallowed_heads_kernel(tc, hid, voc_words, voc_scales, target, b
         held = ctx.enter_context(tc.tile_pool(name="held", bufs=1))
         psum = ctx.enter_context(tc.psum_pool(name="psum", bufs=1))
 
-        def wide(name):
-            return held.tile([P, V], F32, name=name)
-
-        def listed(name):
-            return held.tile([P, I], F32, name=name)
-
-        def column(name):
-            return held.tile([P, 1], F32, name=name)
+        def columns(name, width, tag=None):
+            return held.tile([P, width], F32, name=name, tag=tag or name, align_bytes=64)
 
         list1 = held.tile([P, I // 16], U16, name="list1")
         list2 = held.tile([P, I // 16], U16, name="list2")
         hid_raw = held.tile([P, PACK, Q], F32, name="hid_raw")
-        word_cuts = [(0, 1024), (1024, 2048)]
-        words = [held.tile([P, 2 * (c1 - c0)], U8, name="words%d" % c0, tag="words%d" % c0, align_bytes=64) for c0, c1 in word_cuts]
+        words = [held.tile([P, 2 * (end - first)], U8, name="words%d" % first, align_bytes=64) for first, end in WORD_LOADS]
         voc_plane = held.tile([P, V], U8, name="voc_plane", align_bytes=64)
-
         nc.sync.dma_start(out=hid_raw[:], in_=hid.rearrange("(p t) q -> p t q", t=PACK))
-        for quad in range(4):
+        for quadrant in range(4):
             nc.sync.dma_start(
-                out=voc_plane[32 * quad : 32 * quad + 4, :].bitcast(I32),
-                in_=voc_scales[0, 4 * quad : 4 * quad + 4, :].bitcast(I32),
+                out=voc_plane[32 * quadrant : 32 * quadrant + 4, :].bitcast(I32),
+                in_=voc_scales[0, 4 * quadrant : 4 * quadrant + 4, :].bitcast(I32),
             )
-        for tile, (c0, c1) in zip(words, word_cuts):
-            nc.sync.dma_start(out=tile[:].bitcast(I32), in_=voc_words[0, :, 2 * c0 : 2 * c1].bitcast(I32))
+        for tile, (first, end) in zip(words, WORD_LOADS):
+            nc.sync.dma_start(out=tile[:].bitcast(I32), in_=voc_words[0, :, 2 * first : 2 * end].bitcast(I32))
         nc.sync.dma_start(list1[:], offs)
         nc.sync.dma_start(list2[:], offs2)
+        base_sb = columns("base_sb", V)
+        nc.sync.dma_start(out=base_sb[:], in_=base)
+        target_sb = columns("target_sb", I)
+        nc.sync.dma_start(out=target_sb[:], in_=target)
 
-        warm = column("warm")
-        nc.vector.memset(warm[:], 0.0)
-        warm_out = column("warm_out")
-        nc.scalar.activation(warm_out[:], warm[:], ACT.Exp)
+        zero = columns("zero", 1)
+        nc.vector.memset(zero[:], 0.0)
+        minus_one = columns("minus_one", 1)
+        nc.scalar.activation(minus_one[:], zero[:], ACT.Copy, bias=-1.0)
 
-        window1 = wide("window1")
+        window1 = columns("window1", V)
         nc.vector.memset(window1[:].bitcast(U32), 0)
-        identity = held.tile([P, P], F32, name="identity")
+        identity = columns("identity", P)
         make_identity(nc, identity[:])
 
-        grouped = held.tile([P, Q, PACK], BF16, name="grouped", tag="grouped_then_window", align_bytes=64)
+        grouped = held.tile([P, Q, PACK], BF16, name="grouped", tag="grouped_then_window2", align_bytes=64)
         nc.vector.tensor_copy(out=grouped[:], in_=hid_raw[:].rearrange("p t q -> p q t"))
-        hid_codes = held.tile([P, Q], U32, name="hid_codes", tag="codes_then_target", align_bytes=64)
+        hid_codes = held.tile([P, Q], U32, name="hid_codes", align_bytes=64)
         hid_plane = held.tile([P, Q], U8, name="hid_plane", align_bytes=64)
         nc.vector.quantize_mx(
             out=hid_codes[:].bitcast(FP8X4), scales=hid_plane[:], in_=grouped[:].rearrange("p q t -> p (q t)")
         )
-
-        window2 = held.tile([P, V], F32, name="window2", tag="grouped_then_window", align_bytes=64)
+        window2 = columns("window2", V, "grouped_then_window2")
         nc.vector.memset(window2[:].bitcast(U32), 0)
 
-        upright = [psum.tile([P, BANK], F32, name="upright%d" % j) for j in range(BANKS)]
-        turned = [psum.tile([P, BANK], F32, name="turned%d" % j) for j in range(BANKS)]
-        a = wide("a")
+        upright = [psum.tile([P, BANK], F32, name="upright%d" % j) for j in range(V // BANK)]
+        turned = [psum.tile([P, BANK], F32, name="turned%d" % j) for j in range(V // BANK)]
+
+        def turn_in(source, j, blocks, bank, opens, closes):
+            for b in range(blocks):
+                first = j * BANK + b * P
+                nc.tensor.matmul(
+                    bank[:, b * P : (b + 1) * P], source[:, first : first + P], identity[:],
+                    start=(opens and b == 0), stop=(closes and b == blocks - 1), is_transpose=True,
+                )
+
+        def turn_back(j, blocks, bank, staged):
+            nc.scalar.copy(staged[:, j * BANK : j * BANK + blocks * P], bank[:, : blocks * P])
+            for b in range(blocks):
+                first = j * BANK + b * P
+                nc.tensor.transpose(upright[j][:, b * P : (b + 1) * P], staged[:, first : first + P], identity[:])
+
+        a = columns("a", V)
         passes = [
-            (0, 512, 0, upright[0], "scalar"),
-            (512, 512, 0, upright[1], "scalar"),
-            (1024, 512, 1, upright[2], "vector"),
-            (1536, 256, 1, upright[3], "scalar"),
-            (1792, 256, 1, turned[3], "vector"),
+            (0, 512, 0, upright[0], nc.scalar.copy),
+            (512, 512, 1, upright[1], nc.scalar.copy),
+            (1024, 512, 2, upright[2], nc.vector.tensor_copy),
+            (1536, 256, 2, upright[3], nc.scalar.copy),
+            (1792, 256, 2, turned[3], nc.vector.tensor_copy),
         ]
-        for c0, width, piece, bank, engine in passes:
-            w0 = 2 * (c0 - word_cuts[piece][0])
+        for first, width, load, bank, copy_out in passes:
+            byte = 2 * (first - WORD_LOADS[load][0])
             nc.tensor.matmul_mx(
                 out=bank[:, :width],
                 lhsT=hid_codes[:].bitcast(FP8X4),
                 lhsT_scale=hid_plane[:],
-                rhs=words[piece][:, w0 : w0 + 2 * width].bitcast(FP4X4),
-                rhs_scale=voc_plane[:, c0 : c0 + width],
+                rhs=words[load][:, byte : byte + 2 * width].bitcast(FP4X4),
+                rhs_scale=voc_plane[:, first : first + width],
                 start=True,
                 stop=True,
             )
-            if engine == "scalar":
-                nc.scalar.copy(a[:, c0 : c0 + width], bank[:, :width])
-            else:
-                nc.vector.tensor_copy(a[:, c0 : c0 + width], bank[:, :width])
+            copy_out(a[:, first : first + width], bank[:, :width])
 
-        tgt = held.tile([P, I], F32, name="tgt", tag="codes_then_target", align_bytes=64)
-        nc.sync.dma_start(out=tgt[:], in_=target)
-        base_sb = held.tile([P, V], F32, name="base_sb", tag="words1024", align_bytes=64)
-        nc.sync.dma_start(out=base_sb[:], in_=base)
+        for j, blocks in enumerate(OUT_BLOCKS):
+            turn_in(base_sb, j, blocks, turned[j], True, False)
 
-        a1 = listed("a1")
-        a2 = held.tile([P, I], F32, name="a2", tag="a2_then_staged")
-        neg_max = column("neg_max")
+        a1 = columns("a1", I)
+        a2 = columns("a2", I, "a2_then_staged")
+        neg_max = columns("neg_max", 1)
         nc.vector.tensor_copy(a1[:], a[:].indirect(list1[:]))
         nc.vector.tensor_reduce(neg_max[:], a1[:], mybir.AxisListType.X, ALU.max, negate=True)
         nc.vector.tensor_copy(a2[:], a[:].indirect(list2[:]))
-
-        p = held.tile([P, I], F32, name="p", tag="p_then_staged")
-        z = column("z")
+        p = columns("p", I, "p_then_staged")
+        z = columns("z", 1)
         nc.scalar.activation(p[:], a1[:], ACT.Exp, bias=neg_max[:], accum_out=z[:])
         nc.vector.tensor_copy(window1[:].indirect(list1[:]), p[:])
 
-        def turn_in(source, j, opens, closes, blocks=BLOCKS):
-            for b in range(blocks):
-                c0 = j * BANK + b * P
-                nc.tensor.matmul(
-                    turned[j][:, b * P : (b + 1) * P], source[:, c0 : c0 + P], identity[:],
-                    start=(opens and b == 0), stop=(closes and b == blocks - 1), is_transpose=True,
-                )
-
-        def turn_back(j, staged, blocks=BLOCKS):
-            nc.scalar.copy(staged[:, j * BANK : j * BANK + blocks * P], turned[j][:, : blocks * P])
-            for b in range(blocks):
-                c0 = j * BANK + b * P
-                nc.tensor.transpose(upright[j][:, b * P : (b + 1) * P], staged[:, c0 : c0 + P], identity[:])
-
-        k1 = column("k1")
-        nc.scalar.activation(k1[:], neg_max[:], ACT.Copy, scale=0.5, bias=-0.25)
+        shift_a = columns("shift_a", 1)
+        nc.scalar.activation(shift_a[:], neg_max[:], ACT.Copy, scale=0.5, bias=-0.25)
         z_bits = z[:].bitcast(U32)
-        exp0 = column("exp0")
+        exp0 = columns("exp0", 1)
         nc.scalar.activation(exp0[:], z_bits, ACT.Exp, scale=-BITS_SLOPE, bias=BITS_OFFSET)
-        zq = column("zq")
-        nc.scalar.activation(zq[:], z[:], ACT.Copy, scale=0.5 / 512.0)
-        n0 = column("n0")
-        nc.scalar.activation(n0[:], z_bits, ACT.Copy, scale=-BITS_SLOPE, bias=BITS_OFFSET - 0.5)
-        h0 = column("h0")
-        nc.scalar.activation(h0[:], exp0[:], ACT.Square, scale=zq[:], bias=-1.0)
-        k2 = column("k2")
-        nc.scalar.activation(k2[:], n0[:], ACT.Identity, scale=0.5, bias=k1[:])
-        exp1 = column("exp1")
-        nc.scalar.activation(exp1[:], h0[:], ACT.Exp, scale=2.0, bias=n0[:])
-        k3 = column("k3")
-        nc.scalar.activation(k3[:], h0[:], ACT.Identity, bias=k2[:])
-        h1 = column("h1")
-        nc.scalar.activation(h1[:], exp1[:], ACT.Square, scale=zq[:], bias=-1.0)
-        neg_z = held.tile([P, 1], F32, name="neg_z", tag="neg_z_then_half_r")
+        z_1024th = columns("z_1024th", 1)
+        nc.scalar.activation(z_1024th[:], z[:], ACT.Copy, scale=0.5 / B_FACTOR)
+        neg_guess = columns("neg_guess", 1)
+        nc.scalar.activation(neg_guess[:], z_bits, ACT.Copy, scale=-BITS_SLOPE, bias=BITS_OFFSET - 0.5)
+        square0 = columns("square0", 1)
+        nc.scalar.activation(square0[:], exp0[:], ACT.Square, scale=z_1024th[:], bias=minus_one[:])
+        shift_b = columns("shift_b", 1)
+        nc.scalar.activation(shift_b[:], neg_guess[:], ACT.Identity, scale=0.5, bias=shift_a[:])
+        exp1 = columns("exp1", 1)
+        nc.scalar.activation(exp1[:], square0[:], ACT.Exp, scale=2.0, bias=neg_guess[:])
+        shift_c = columns("shift_c", 1)
+        nc.scalar.activation(shift_c[:], square0[:], ACT.Identity, bias=shift_b[:])
+        square1 = columns("square1", 1)
+        nc.scalar.activation(square1[:], exp1[:], ACT.Square, scale=z_1024th[:], bias=minus_one[:])
+        neg_z = columns("neg_z", 1, "neg_z_then_half_r")
         nc.scalar.activation(neg_z[:], z[:], ACT.Copy, scale=-1.0)
-        shift = column("shift")
-        nc.scalar.activation(shift[:], h1[:], ACT.Identity, bias=k3[:])
-        th = listed("th")
+        shift = columns("shift", 1)
+        nc.scalar.activation(shift[:], square1[:], ACT.Identity, bias=shift_c[:])
+        th = columns("th", I)
         nc.scalar.activation(th[:], a2[:], ACT.Tanh, scale=0.5, bias=shift[:])
 
-        e1x2 = listed("e1x2")
-        sum_e1x2 = column("sum_e1x2")
-        nc.vector.scalar_tensor_tensor(e1x2[:], th[:], 1.0, tgt[:], ALU.add, ALU.mult, accum_out=sum_e1x2[:])
-        neg_rz = column("neg_rz")
+        e1x2 = columns("e1x2", I)
+        sum_e1x2 = columns("sum_e1x2", 1)
+        nc.vector.scalar_tensor_tensor(e1x2[:], th[:], 1.0, target_sb[:], ALU.add, ALU.mult, accum_out=sum_e1x2[:])
+        neg_rz = columns("neg_rz", 1)
         nc.vector.reciprocal(neg_rz[:], neg_z[:])
         nc.vector.tensor_copy(window2[:].indirect(list2[:]), e1x2[:])
 
-        half_r = held.tile([P, I], F32, name="half_r", tag="neg_z_then_half_r")
+        half_r = columns("half_r", I, "neg_z_then_half_r")
         nc.scalar.activation(half_r[:], th[:], ACT.Identity, scale=-0.25, bias=0.25)
-        w = listed("w")
+        w = columns("w", I)
         nc.gpsimd.tensor_tensor(w[:], e1x2[:], half_r[:], ALU.mult)
-        dz_x2 = column("dz_x2")
+        dz_x2 = columns("dz_x2", 1)
         nc.scalar.activation(dz_x2[:], sum_e1x2[:], ACT.Copy, scale=neg_rz[:])
-        sum_e1 = column("sum_e1")
+        sum_e1 = columns("sum_e1", 1)
         nc.scalar.activation(sum_e1[:], sum_e1x2[:], ACT.Copy, scale=0.5)
 
-        hda_blocks = [4, 4, 3]
-        staged_p = held.tile([P, sum(hda_blocks) * P], F32, name="staged_p", tag="a2_then_staged")
-        for j, n in enumerate(hda_blocks):
-            turn_in(window1, j, True, True, n)
-        for j, n in enumerate(hda_blocks):
-            turn_back(j, staged_p, n)
-
-        hda = wide("hda")
-        last = slice(sum(hda_blocks) * P, V)
-        s2_last = held.tile([P, V - sum(hda_blocks) * P], F32, name="s2_last")
-        nc.scalar.activation(s2_last[:], window1[:, last], ACT.Copy, scale=dz_x2[:])
-        nc.gpsimd.tensor_tensor(hda[:, last], s2_last[:], window2[:, last], ALU.add)
-        for j, n in enumerate(hda_blocks):
-            cols = slice(j * BANK, j * BANK + n * P)
-            nc.vector.scalar_tensor_tensor(hda[:, cols], upright[j][:, : n * P], dz_x2[:], window2[:, cols], ALU.mult, ALU.add)
-        dz = column("dz")
+        hda_split = sum(HDA_BLOCKS) * P
+        staged_p = columns("staged_p", hda_split, "a2_then_staged")
+        for j, blocks in enumerate(HDA_BLOCKS):
+            turn_in(window1, j, blocks, upright[j], True, True)
+        for j, blocks in enumerate(HDA_BLOCKS):
+            turn_back(j, blocks, upright[j], staged_p)
+        hda = columns("hda", V)
+        s2x2_rest = columns("s2x2_rest", V - hda_split)
+        nc.scalar.activation(s2x2_rest[:], window1[:, hda_split:], ACT.Copy, scale=dz_x2[:])
+        nc.gpsimd.tensor_tensor(hda[:, hda_split:], s2x2_rest[:], window2[:, hda_split:], ALU.add)
+        for j, blocks in enumerate(HDA_BLOCKS):
+            cols = slice(j * BANK, j * BANK + blocks * P)
+            nc.vector.scalar_tensor_tensor(
+                hda[:, cols], upright[j][:, : blocks * P], dz_x2[:], window2[:, cols], ALU.mult, ALU.add
+            )
+        dz = columns("dz", 1)
         nc.scalar.activation(dz[:], dz_x2[:], ACT.Copy, scale=0.5)
-        blocks = [4, 4, 4, 1]
-        for j in range(BANKS):
-            turn_in(base_sb, j, True, False, blocks[j])
 
-        he2_p = listed("he2_p")
+        he2_p = columns("he2_p", I)
         nc.vector.tensor_tensor(he2_p[:], hda[:].indirect(list1[:]), p[:], ALU.mult)
-        he1_w = listed("he1_w")
+        he1_w = columns("he1_w", I)
         nc.vector.tensor_tensor(he1_w[:], hda[:].indirect(list2[:]), w[:], ALU.mult)
-
-        neg_he2_pn = listed("neg_he2_pn")
-        neg_h = column("neg_h")
-        nc.scalar.activation(neg_he2_pn[:], he2_p[:], ACT.Copy, scale=neg_rz[:], accum_out=neg_h[:])
-        he2_dz_p = listed("he2_dz_p")
-        nc.scalar.activation(he2_dz_p[:], neg_he2_pn[:], ACT.Copy, scale=sum_e1[:])
-        hz_part = column("hz_part")
-        nc.scalar.activation(hz_part[:], neg_h[:], ACT.Copy, scale=dz[:])
-        e5 = listed("e5")
-        sum_e5 = column("sum_e5")
+        neg_he2_p_rz = columns("neg_he2_p_rz", I)
+        neg_h = columns("neg_h", 1)
+        nc.scalar.activation(neg_he2_p_rz[:], he2_p[:], ACT.Copy, scale=neg_rz[:], accum_out=neg_h[:])
+        he2_dz_p = columns("he2_dz_p", I)
+        nc.scalar.activation(he2_dz_p[:], neg_he2_p_rz[:], ACT.Copy, scale=sum_e1[:])
+        neg_h_dz = columns("neg_h_dz", 1)
+        nc.scalar.activation(neg_h_dz[:], neg_h[:], ACT.Copy, scale=dz[:])
+        e5 = columns("e5", I)
+        sum_e5 = columns("sum_e5", 1)
         nc.vector.scalar_tensor_tensor(e5[:], w[:], neg_h[:], he1_w[:], ALU.mult, ALU.add, accum_out=sum_e5[:])
         nc.vector.tensor_copy(window2[:].indirect(list2[:]), e5[:])
-        hz = column("hz")
-        nc.scalar.activation(hz[:], sum_e5[:], ACT.Identity, scale=neg_rz[:], bias=hz_part[:])
-        hz_p = listed("hz_p")
+
+        hz = columns("hz", 1)
+        nc.scalar.activation(hz[:], sum_e5[:], ACT.Identity, scale=neg_rz[:], bias=neg_h_dz[:])
+        hz_p = columns("hz_p", I)
         nc.scalar.activation(hz_p[:], p[:], ACT.Copy, scale=hz[:])
         nc.vector.tensor_tensor(window1[:].indirect(list1[:]), he2_dz_p[:], hz_p[:], ALU.add)
 
-        staged_sum = held.tile([P, V], F32, name="staged_sum", tag="p_then_staged")
-        for j in range(BANKS):
-            turn_in(window2, j, False, True, blocks[j])
-        for j in range(BANKS):
-            turn_back(j, staged_sum, blocks[j])
-        tail = slice(sum(blocks) * P, V)
-        tail_width = V - sum(blocks) * P
-        tail_sum = held.tile([P, tail_width], F32, name="tail_sum")
-        nc.gpsimd.tensor_tensor(tail_sum[:], window2[:, tail], base_sb[:, tail], ALU.add)
-        tail_out = held.tile([P, tail_width], F32, name="tail_out")
-        nc.gpsimd.tensor_tensor(tail_out[:], tail_sum[:], window1[:, tail], ALU.add)
-        pieces = [(0, 256), (256, 256), (512, 512), (1024, 512), (1536, 128)]
-        for n, (c0, width) in enumerate(pieces):
-            result = held.tile([P, width], F32, name="result%d" % n)
-            cols = slice(c0, c0 + width)
-            nc.vector.tensor_tensor(result[:], upright[c0 // BANK][:, c0 % BANK : c0 % BANK + width], window1[:, cols], ALU.add)
+        out_split = sum(OUT_BLOCKS) * P
+        staged_sum = columns("staged_sum", out_split, "p_then_staged")
+        for j, blocks in enumerate(OUT_BLOCKS):
+            turn_in(window2, j, blocks, turned[j], False, True)
+        for j, blocks in enumerate(OUT_BLOCKS):
+            turn_back(j, blocks, turned[j], staged_sum)
+        rest_sum = columns("rest_sum", V - out_split)
+        nc.gpsimd.tensor_tensor(rest_sum[:], window2[:, out_split:], base_sb[:, out_split:], ALU.add)
+        rest_out = columns("rest_out", V - out_split)
+        nc.gpsimd.tensor_tensor(rest_out[:], rest_sum[:], window1[:, out_split:], ALU.add)
+        for n, (first, width) in enumerate(OUT_PIECES):
+            piece = columns("piece%d" % n, width)
+            cols = slice(first, first + width)
+            in_bank = slice(first % BANK, first % BANK + width)
+            nc.vector.tensor_tensor(piece[:], upright[first // BANK][:, in_bank], window1[:, cols], ALU.add)
             queue = nc.sync if n % 2 == 0 else nc.scalar
-            queue.dma_start(out=out[:, cols], in_=result[:])
-        nc.scalar.dma_start(out=out[:, tail], in_=tail_out[:])
+            queue.dma_start(out=out[:, cols], in_=piece[:])
+        nc.scalar.dma_start(out=out[:, out_split:], in_=rest_out[:])

import math
from contextlib import ExitStack

import concourse.mybir as mybir
from concourse.masks import make_identity

D, V, Q, I = 512, 2048, 128, 512
FLOPS = 2 * D * Q * V

F32 = mybir.dt.float32
BF16 = mybir.dt.bfloat16
I32 = mybir.dt.int32
U32 = mybir.dt.uint32
U16 = mybir.dt.uint16
U8 = mybir.dt.uint8
FP8X4 = mybir.dt.float8_e4m3fn_x4
FP4X4 = mybir.dt.float4_e2m1fn_x4
ALU = mybir.AluOpType
ACT = mybir.ActivationFunctionType

P = 128
PACK = 4
BANK = 512
B_FACTOR = 512.0

BITS_SLOPE = math.log(2.0) / 2.0**23
BITS_OFFSET = math.log(2.0) * (127.0 - 0.043) + math.log(B_FACTOR)

WORD_LOADS = [(0, 512), (512, 1024), (1024, 2048)]
HDA_BLOCKS = [4, 4, 3]
OUT_BLOCKS = [4, 4, 4, 1]
OUT_PIECES = [(0, 256), (256, 256), (512, 512), (1024, 512), (1536, 128)]


def tile_attend_gpallowed_heads_kernel(tc, hid, voc_words, voc_scales, target, base, offs, offs2, out):
    nc = tc.nc
    with ExitStack() as ctx:
        held = ctx.enter_context(tc.tile_pool(name="held", bufs=1))
        psum = ctx.enter_context(tc.psum_pool(name="psum", bufs=1))

        def columns(name, width, tag=None):
            return held.tile([P, width], F32, name=name, tag=tag or name, align_bytes=64)

        list1 = held.tile([P, I // 16], U16, name="list1")
        list2 = held.tile([P, I // 16], U16, name="list2")
        hid_raw = held.tile([P, PACK, Q], F32, name="hid_raw")
        words = [held.tile([P, 2 * (end - first)], U8, name="words%d" % first, align_bytes=64) for first, end in WORD_LOADS]
        voc_plane = held.tile([P, V], U8, name="voc_plane", align_bytes=64)
        nc.sync.dma_start(out=hid_raw[:], in_=hid.rearrange("(p t) q -> p t q", t=PACK))
        for quadrant in range(4):
            nc.sync.dma_start(
                out=voc_plane[32 * quadrant : 32 * quadrant + 4, :].bitcast(I32),
                in_=voc_scales[0, 4 * quadrant : 4 * quadrant + 4, :].bitcast(I32),
            )
        for tile, (first, end) in zip(words, WORD_LOADS):
            nc.sync.dma_start(out=tile[:].bitcast(I32), in_=voc_words[0, :, 2 * first : 2 * end].bitcast(I32))
        nc.sync.dma_start(list1[:], offs)
        nc.sync.dma_start(list2[:], offs2)
        base_sb = columns("base_sb", V)
        nc.sync.dma_start(out=base_sb[:], in_=base)
        target_sb = columns("target_sb", I)
        nc.sync.dma_start(out=target_sb[:], in_=target)

        zero = columns("zero", 1)
        nc.vector.memset(zero[:], 0.0)
        minus_one = columns("minus_one", 1)
        nc.scalar.activation(minus_one[:], zero[:], ACT.Copy, bias=-1.0)

        window1 = columns("window1", V)
        nc.vector.memset(window1[:].bitcast(U32), 0)
        identity = columns("identity", P)
        make_identity(nc, identity[:])

        grouped = held.tile([P, Q, PACK], BF16, name="grouped", tag="grouped_then_window2", align_bytes=64)
        nc.vector.tensor_copy(out=grouped[:], in_=hid_raw[:].rearrange("p t q -> p q t"))
        hid_codes = held.tile([P, Q], U32, name="hid_codes", align_bytes=64)
        hid_plane = held.tile([P, Q], U8, name="hid_plane", align_bytes=64)
        nc.vector.quantize_mx(
            out=hid_codes[:].bitcast(FP8X4), scales=hid_plane[:], in_=grouped[:].rearrange("p q t -> p (q t)")
        )
        window2 = columns("window2", V, "grouped_then_window2")
        nc.vector.memset(window2[:].bitcast(U32), 0)

        upright = [psum.tile([P, BANK], F32, name="upright%d" % j) for j in range(V // BANK)]
        turned = [psum.tile([P, BANK], F32, name="turned%d" % j) for j in range(V // BANK)]

        def turn_in(source, j, blocks, bank, opens, closes):
            for b in range(blocks):
                first = j * BANK + b * P
                nc.tensor.matmul(
                    bank[:, b * P : (b + 1) * P], source[:, first : first + P], identity[:],
                    start=(opens and b == 0), stop=(closes and b == blocks - 1), is_transpose=True,
                )

        def turn_back(j, blocks, bank, staged):
            nc.scalar.copy(staged[:, j * BANK : j * BANK + blocks * P], bank[:, : blocks * P])
            for b in range(blocks):
                first = j * BANK + b * P
                nc.tensor.transpose(upright[j][:, b * P : (b + 1) * P], staged[:, first : first + P], identity[:])

        a = columns("a", V)
        passes = [
            (0, 512, 0, upright[0], nc.scalar.copy),
            (512, 512, 1, upright[1], nc.scalar.copy),
            (1024, 512, 2, upright[2], nc.vector.tensor_copy),
            (1536, 256, 2, upright[3], nc.scalar.copy),
            (1792, 256, 2, turned[3], nc.vector.tensor_copy),
        ]
        for first, width, load, bank, copy_out in passes:
            byte = 2 * (first - WORD_LOADS[load][0])
            nc.tensor.matmul_mx(
                out=bank[:, :width],
                lhsT=hid_codes[:].bitcast(FP8X4),
                lhsT_scale=hid_plane[:],
                rhs=words[load][:, byte : byte + 2 * width].bitcast(FP4X4),
                rhs_scale=voc_plane[:, first : first + width],
                start=True,
                stop=True,
            )
            copy_out(a[:, first : first + width], bank[:, :width])

        for j, blocks in enumerate(OUT_BLOCKS):
            turn_in(base_sb, j, blocks, turned[j], True, False)

        a1 = columns("a1", I)
        a2 = columns("a2", I, "a2_then_staged")
        neg_max = columns("neg_max", 1)
        nc.vector.tensor_copy(a1[:], a[:].indirect(list1[:]))
        nc.vector.tensor_reduce(neg_max[:], a1[:], mybir.AxisListType.X, ALU.max, negate=True)
        nc.vector.tensor_copy(a2[:], a[:].indirect(list2[:]))
        p = columns("p", I, "p_then_staged")
        z = columns("z", 1)
        nc.scalar.activation(p[:], a1[:], ACT.Exp, bias=neg_max[:], accum_out=z[:])
        nc.vector.tensor_copy(window1[:].indirect(list1[:]), p[:])

        shift_a = columns("shift_a", 1)
        nc.scalar.activation(shift_a[:], neg_max[:], ACT.Copy, scale=0.5, bias=-0.25)
        z_bits = z[:].bitcast(U32)
        exp0 = columns("exp0", 1)
        nc.scalar.activation(exp0[:], z_bits, ACT.Exp, scale=-BITS_SLOPE, bias=BITS_OFFSET)
        z_1024th = columns("z_1024th", 1)
        nc.scalar.activation(z_1024th[:], z[:], ACT.Copy, scale=0.5 / B_FACTOR)
        neg_guess = columns("neg_guess", 1)
        nc.scalar.activation(neg_guess[:], z_bits, ACT.Copy, scale=-BITS_SLOPE, bias=BITS_OFFSET - 0.5)
        square0 = columns("square0", 1)
        nc.scalar.activation(square0[:], exp0[:], ACT.Square, scale=z_1024th[:], bias=minus_one[:])
        shift_b = columns("shift_b", 1)
        nc.scalar.activation(shift_b[:], neg_guess[:], ACT.Identity, scale=0.5, bias=shift_a[:])
        exp1 = columns("exp1", 1)
        nc.scalar.activation(exp1[:], square0[:], ACT.Exp, scale=2.0, bias=neg_guess[:])
        shift_c = columns("shift_c", 1)
        nc.scalar.activation(shift_c[:], square0[:], ACT.Identity, bias=shift_b[:])
        square1 = columns("square1", 1)
        nc.scalar.activation(square1[:], exp1[:], ACT.Square, scale=z_1024th[:], bias=minus_one[:])
        neg_z = columns("neg_z", 1, "neg_z_then_half_r")
        nc.scalar.activation(neg_z[:], z[:], ACT.Copy, scale=-1.0)
        shift = columns("shift", 1)
        nc.scalar.activation(shift[:], square1[:], ACT.Identity, bias=shift_c[:])
        th = columns("th", I)
        nc.scalar.activation(th[:], a2[:], ACT.Tanh, scale=0.5, bias=shift[:])

        e1x2 = columns("e1x2", I)
        sum_e1x2 = columns("sum_e1x2", 1)
        nc.vector.scalar_tensor_tensor(e1x2[:], th[:], 1.0, target_sb[:], ALU.add, ALU.mult, accum_out=sum_e1x2[:])
        neg_rz = columns("neg_rz", 1)
        nc.vector.reciprocal(neg_rz[:], neg_z[:])
        nc.vector.tensor_copy(window2[:].indirect(list2[:]), e1x2[:])

        half_r = columns("half_r", I, "neg_z_then_half_r")
        nc.scalar.activation(half_r[:], th[:], ACT.Identity, scale=-0.25, bias=0.25)
        w = columns("w", I)
        nc.gpsimd.tensor_tensor(w[:], e1x2[:], half_r[:], ALU.mult)
        dz_x2 = columns("dz_x2", 1)
        nc.scalar.activation(dz_x2[:], sum_e1x2[:], ACT.Copy, scale=neg_rz[:])
        sum_e1 = columns("sum_e1", 1)
        nc.scalar.activation(sum_e1[:], sum_e1x2[:], ACT.Copy, scale=0.5)

        hda_split = sum(HDA_BLOCKS) * P
        staged_p = columns("staged_p", hda_split, "a2_then_staged")
        for j, blocks in enumerate(HDA_BLOCKS):
            turn_in(window1, j, blocks, upright[j], True, True)
        for j, blocks in enumerate(HDA_BLOCKS):
            turn_back(j, blocks, upright[j], staged_p)
        hda = columns("hda", V)
        s2x2_rest = columns("s2x2_rest", V - hda_split)
        nc.scalar.activation(s2x2_rest[:], window1[:, hda_split:], ACT.Copy, scale=dz_x2[:])
        nc.gpsimd.tensor_tensor(hda[:, hda_split:], s2x2_rest[:], window2[:, hda_split:], ALU.add)
        for j, blocks in enumerate(HDA_BLOCKS):
            cols = slice(j * BANK, j * BANK + blocks * P)
            nc.vector.scalar_tensor_tensor(
                hda[:, cols], upright[j][:, : blocks * P], dz_x2[:], window2[:, cols], ALU.mult, ALU.add
            )
        dz = columns("dz", 1)
        nc.scalar.activation(dz[:], dz_x2[:], ACT.Copy, scale=0.5)

        he2_p = columns("he2_p", I)
        nc.vector.tensor_tensor(he2_p[:], hda[:].indirect(list1[:]), p[:], ALU.mult)
        he1_w = columns("he1_w", I)
        nc.vector.tensor_tensor(he1_w[:], hda[:].indirect(list2[:]), w[:], ALU.mult)
        neg_he2_p_rz = columns("neg_he2_p_rz", I)
        neg_h = columns("neg_h", 1)
        nc.scalar.activation(neg_he2_p_rz[:], he2_p[:], ACT.Copy, scale=neg_rz[:], accum_out=neg_h[:])
        he2_dz_p = columns("he2_dz_p", I)
        nc.scalar.activation(he2_dz_p[:], neg_he2_p_rz[:], ACT.Copy, scale=sum_e1[:])
        neg_h_dz = columns("neg_h_dz", 1)
        nc.scalar.activation(neg_h_dz[:], neg_h[:], ACT.Copy, scale=dz[:])
        e5 = columns("e5", I)
        sum_e5 = columns("sum_e5", 1)
        nc.vector.scalar_tensor_tensor(e5[:], w[:], neg_h[:], he1_w[:], ALU.mult, ALU.add, accum_out=sum_e5[:])
        nc.vector.tensor_copy(window2[:].indirect(list2[:]), e5[:])

        hz = columns("hz", 1)
        nc.scalar.activation(hz[:], sum_e5[:], ACT.Identity, scale=neg_rz[:], bias=neg_h_dz[:])
        hz_p = columns("hz_p", I)
        nc.scalar.activation(hz_p[:], p[:], ACT.Copy, scale=hz[:])
        nc.vector.tensor_tensor(window1[:].indirect(list1[:]), he2_dz_p[:], hz_p[:], ALU.add)

        out_split = sum(OUT_BLOCKS) * P
        staged_sum = columns("staged_sum", out_split, "p_then_staged")
        for j, blocks in enumerate(OUT_BLOCKS):
            turn_in(window2, j, blocks, turned[j], False, True)
        for j, blocks in enumerate(OUT_BLOCKS):
            turn_back(j, blocks, turned[j], staged_sum)
        rest_sum = columns("rest_sum", V - out_split)
        nc.gpsimd.tensor_tensor(rest_sum[:], window2[:, out_split:], base_sb[:, out_split:], ALU.add)
        rest_out = columns("rest_out", V - out_split)
        nc.gpsimd.tensor_tensor(rest_out[:], rest_sum[:], window1[:, out_split:], ALU.add)
        for n, (first, width) in enumerate(OUT_PIECES):
            piece = columns("piece%d" % n, width)
            cols = slice(first, first + width)
            in_bank = slice(first % BANK, first % BANK + width)
            nc.vector.tensor_tensor(piece[:], upright[first // BANK][:, in_bank], window1[:, cols], ALU.add)
            queue = nc.sync if n % 2 == 0 else nc.scalar
            queue.dma_start(out=out[:, cols], in_=piece[:])
        nc.scalar.dma_start(out=out[:, out_split:], in_=rest_out[:])
